import numpy as np
import ml_dtypes


def mxq(x, axis, fmt="e4m3"):
    dtype, down = {"e4m3": (ml_dtypes.float8_e4m3fn, 7), "e5m2": (ml_dtypes.float8_e5m2, 14)}[fmt]
    v = np.moveaxis(np.asarray(x, np.float32).astype(ml_dtypes.bfloat16).astype(np.float64), axis, -1)
    blocks = v.reshape(v.shape[:-1] + (-1, 32))
    amax = np.abs(blocks).max(-1, keepdims=True)
    byte = np.maximum(np.where(amax > 0, np.frexp(amax)[1] - 1 + 127, 0) - down, 1)
    scale = np.exp2(byte - 127.0)
    codes = (blocks / scale).astype(np.float32).astype(dtype).astype(np.float64)
    return np.moveaxis((codes * scale).reshape(v.shape), -1, axis)


WIDE = False


def mx_kscale(k):
    if not WIDE:
        return np.ones(k)
    levels = np.array([10, -10, 5, -5, 0])
    if k % 512:
        return np.exp2(np.random.permutation(np.resize(levels, k // 32))).repeat(32)
    a = np.empty((k // 512, 16))
    for p in range(k // 512):
        a[p, :8] = np.random.permutation(np.resize(levels, 8))
        for g in range(8):
            far = levels[np.abs(levels - a[p, g]) >= 10]
            a[p, g + 8] = far[np.random.randint(len(far))]
    return np.exp2(a.ravel()).repeat(32)


def f64(x):
    return np.asarray(x).astype(np.float64)


def split(x):
    m, e = np.frexp(f64(x))
    hi = np.ldexp(np.trunc(16.0 * m) / 16.0, e)
    return hi, f64(x) - hi


def gelu(v):
    return 0.5 * v * (1.0 + np.tanh(np.sqrt(2.0 / np.pi) * (v + 0.044715 * v**3)))


K, M, T = 1024, 512, 1536


def setup_inputs():
    n = np.random.standard_normal
    s = mx_kscale(K)[:, None]
    return {
        "w": (n((K, M)) / np.sqrt(K) / s).astype(np.float32),
        "x": (n((K, T)) * s).astype(np.float32),
        "b": (0.3 * n(512)).astype(np.float32),
    }


def reference(w, x, b):
    w_hi, w_lo = split(w)
    w_hi_, w_lo_ = mxq(w_hi, 0, "e4m3"), mxq(w_lo, 0, "e4m3")
    x_ = mxq(f64(x), 0, "e4m3")
    y = w_hi_.T @ x_ + w_lo_.T @ x_
    return gelu(y + f64(b)[:, None])

@@ -1,0 +1,265 @@
+from contextlib import ExitStack
+
+import concourse.mybir as mybir
+from concourse.masks import make_identity
+
+K, M, T = 1024, 512, 1536
+P = 128
+PACK = 4
+K_PASS = P * PACK
+PASSES = K // K_PASS
+CHUNK = 512
+HALF = 256
+M_TILES = M // P
+GROUPS = [(0, 0, CHUNK), (1, 0, CHUNK), (2, 0, HALF), (2, HALF, CHUNK)]
+HI_MASK = -1048576
+HI_MASK_PAIR = -983056
+
+FLOPS = 2 * 2 * K * M * T
+
+F32 = mybir.dt.float32
+BF16 = mybir.dt.bfloat16
+I32 = mybir.dt.int32
+U32 = mybir.dt.uint32
+U8 = mybir.dt.uint8
+FP8X4 = mybir.dt.float8_e4m3fn_x4
+ALU = mybir.AluOpType
+GELU = mybir.ActivationFunctionType.Gelu_apprx_tanh
+
+
+def rows_view(raw):
+    return raw.rearrange("p t (c i) -> p c t i", i=4)
+
+
+def packed_view(grouped):
+    return grouped.rearrange("p (c i) t -> p c t i", i=4)
+
+
+def tile_mix_hilo_fm_gelu_kernel(tc, w, x, b, out):
+    nc = tc.nc
+    chunks = T // CHUNK
+
+    with ExitStack() as ctx:
+        keep = ctx.enter_context(tc.tile_pool(name="keep", bufs=1))
+        psum = ctx.enter_context(tc.psum_pool(name="psum", bufs=1))
+        ctx.enter_context(tc.manual_schedule())
+
+        w_raw = [keep.tile([P, PACK, M], F32, name="w_raw%d" % kp, align_bytes=64) for kp in range(PASSES)]
+        a_raw = [keep.tile([P, PACK, CHUNK], F32, name="a_raw%d" % kp, align_bytes=64) for kp in range(PASSES)]
+        b_raw = [keep.tile([P, PACK, CHUNK], F32, name="b_raw%d" % kp, align_bytes=64) for kp in range(PASSES)]
+        c_raw = [keep.tile([P, PACK, CHUNK], F32, name="c_raw%d" % kp, align_bytes=64) for kp in range(PASSES)]
+
+        def load_x(tile, kp, t0, t1):
+            nc.sync.dma_start(
+                out=tile[:],
+                in_=x[kp * K_PASS:(kp + 1) * K_PASS, t0:t1].rearrange("(p j) t -> p j t", j=PACK))
+
+        w_rows = [w[kp * K_PASS:(kp + 1) * K_PASS, :].rearrange("(p j) c -> p j c", j=PACK) for kp in range(PASSES)]
+        nc.sync.dma_start(out=w_raw[0][:, 0:2, :], in_=w_rows[0][:, 0:2, :])
+        nc.sync.dma_start(out=w_raw[0][:, 2:4, :], in_=w_rows[0][:, 2:4, :])
+        load_x(a_raw[0], 0, 0, CHUNK)
+        nc.sync.dma_start(out=w_raw[1][:], in_=w_rows[1])
+        load_x(b_raw[0], 0, CHUNK, 2 * CHUNK)
+        load_x(a_raw[1], 1, 0, CHUNK)
+        load_x(b_raw[1], 1, CHUNK, 2 * CHUNK)
+        load_x(c_raw[0], 0, 2 * CHUNK, T)
+        load_x(c_raw[1], 1, 2 * CHUNK, T)
+        x_raw = {(ch, kp): tile[:] for kp in range(PASSES) for ch, tile in enumerate((a_raw[kp], b_raw[kp], c_raw[kp]))}
+
+        warm = keep.tile([P, 1], F32, name="warm")
+        warm_out = keep.tile([P, 1], F32, name="warm_out")
+        b_rows = keep.tile([P, P], F32, name="b_rows")
+        ident = keep.tile([P, P], F32, name="ident")
+        bias = keep.tile([P, M_TILES], F32, name="bias")
+        nc.vector.memset(warm[:], 0.0)
+        nc.gpsimd.memset(b_rows[:], 0.0)
+        make_identity(nc, ident[:])
+        nc.scalar.dma_start(out=b_rows[0:M_TILES, :], in_=b.rearrange("(m p) -> m p", p=P))
+        nc.scalar.activation(out=warm_out[:], in_=warm[:], func=GELU)
+        bT = psum.tile([P, CHUNK], F32, name="bT", tag="acc7")
+
+        hi_f = [keep.tile([P, PACK, M], F32, name="hi_f%d" % kp, align_bytes=64) for kp in range(PASSES)]
+        w_grp = {}
+        w_codes = {}
+        w_scales = {}
+        for kp in range(PASSES):
+            for h in range(2):
+                g = keep.tile([P, 2, HALF, PACK], BF16, name="w_grp%d_%d" % (kp, h), align_bytes=64)
+                c = keep.tile([P, 2, HALF], U32, name="w_codes%d_%d" % (kp, h), align_bytes=64)
+                s = keep.tile([P, 2, HALF], U8, name="w_scales%d_%d" % (kp, h), align_bytes=64)
+                w_grp[(kp, h)] = g
+                w_codes[(kp, h)] = c
+                w_scales[(kp, h)] = s
+        x_grp = {}
+        x_codes = {}
+        x_scales = {}
+        for ch in range(chunks):
+            for kp in range(PASSES):
+                g = keep.tile([P, CHUNK, PACK], BF16, name="x_grp%d_%d" % (ch, kp), align_bytes=64)
+                c = keep.tile([P, CHUNK], U32, name="x_codes%d_%d" % (ch, kp), align_bytes=64)
+                s = keep.tile([P, CHUNK], U8, name="x_scales%d_%d" % (ch, kp), align_bytes=64)
+                x_grp[(ch, kp)] = g
+                x_codes[(ch, kp)] = c
+                x_scales[(ch, kp)] = s
+
+        def mask(kp, j0, j1, c0=0, c1=M):
+            nc.vector.tensor_scalar(
+                out=hi_f[kp][:, j0:j1, c0:c1].bitcast(I32), in0=w_raw[kp][:, j0:j1, c0:c1].bitcast(I32),
+                scalar1=HI_MASK, scalar2=None, op0=ALU.bitwise_and)
+
+        def hi_copy(copier, kp, h):
+            cols = slice(h * HALF, (h + 1) * HALF)
+            copier(out=packed_view(w_grp[(kp, h)][:, 0, :, :]), in_=rows_view(hi_f[kp][:, :, cols]))
+
+        def lo_sub(kp, h):
+            cols = slice(h * HALF, (h + 1) * HALF)
+            nc.vector.tensor_tensor(
+                out=packed_view(w_grp[(kp, h)][:, 1, :, :]), in0=rows_view(w_raw[kp][:, :, cols]),
+                in1=rows_view(hi_f[kp][:, :, cols]), op=ALU.subtract)
+
+        def trunc_copy(h):
+            top = w_raw[1][:].bitcast(BF16)[:, :, 2 * h * HALF + 1:2 * (h + 1) * HALF:2]
+            nc.scalar.copy(out=packed_view(w_grp[(1, h)][:, 0, :, :]), in_=rows_view(top))
+
+        def mask_pairs(h):
+            words = w_grp[(1, h)][:, 0, :, :].rearrange("p c t -> p (c t)").bitcast(I32)
+            nc.vector.tensor_scalar(out=words, in0=words, scalar1=HI_MASK_PAIR, scalar2=None, op0=ALU.bitwise_and)
+
+        def lo_sub_packed(h):
+            cols = slice(h * HALF, (h + 1) * HALF)
+            nc.vector.tensor_tensor(
+                out=packed_view(w_grp[(1, h)][:, 1, :, :]), in0=rows_view(w_raw[1][:, :, cols]),
+                in1=packed_view(w_grp[(1, h)][:, 0, :, :]), op=ALU.subtract)
+
+        def w_quant(kp, h):
+            nc.vector.quantize_mx(
+                out=w_codes[(kp, h)][:].rearrange("p s c -> p (s c)").bitcast(FP8X4),
+                scales=w_scales[(kp, h)][:].rearrange("p s c -> p (s c)"),
+                in_=w_grp[(kp, h)][:].rearrange("p s c t -> p (s c t)"))
+
+        def x_copy(copier, ch, kp, c0=0, c1=CHUNK):
+            copier(out=packed_view(x_grp[(ch, kp)][:, c0:c1, :]), in_=rows_view(x_raw[(ch, kp)][:, :, c0:c1]))
+
+        def x_quant(ch, kp, c0=0, c1=CHUNK):
+            nc.vector.quantize_mx(
+                out=x_codes[(ch, kp)][:, c0:c1].bitcast(FP8X4), scales=x_scales[(ch, kp)][:, c0:c1],
+                in_=x_grp[(ch, kp)][:, c0:c1, :].rearrange("p c t -> p (c t)"))
+
+        def warm_up(passes):
+            scratch = psum.tile([P, CHUNK], F32, name="scratch", tag="acc6")
+            for i in range(passes):
+                nc.tensor.matmul_mx(
+                    out=scratch[:],
+                    lhsT=w_codes[(0, 0)][:, 0, 0:P].bitcast(FP8X4),
+                    lhsT_scale=w_scales[(0, 0)][:, 0, 0:P],
+                    rhs=w_codes[(0, 0)][:].rearrange("p s c -> p (s c)").bitcast(FP8X4),
+                    rhs_scale=w_scales[(0, 0)][:].rearrange("p s c -> p (s c)"),
+                    start=True, stop=True)
+
+        acc = {}
+
+        def matmuls(group, kp, m):
+            ch, c0, c1 = GROUPS[group]
+            if kp == 0:
+                a = psum.tile([P, c1 - c0], F32, name="acc%d_%d" % (group, m), tag="acc%d" % ((group % 2) * M_TILES + m))
+                acc[(group, m)] = a
+            h = m // 2
+            for part in range(2):
+                cols = slice((m % 2) * P, (m % 2 + 1) * P)
+                nc.tensor.matmul_mx(
+                    out=acc[(group, m)][:],
+                    lhsT=w_codes[(kp, h)][:, part, cols].bitcast(FP8X4),
+                    lhsT_scale=w_scales[(kp, h)][:, part, cols],
+                    rhs=x_codes[(ch, kp)][:, c0:c1].bitcast(FP8X4),
+                    rhs_scale=x_scales[(ch, kp)][:, c0:c1],
+                    start=(kp == 0 and part == 0), stop=(kp == PASSES - 1 and part == 1))
+
+        res = {}
+        for ch in range(chunks):
+            r = keep.tile([P, M_TILES, CHUNK], F32, name="res%d" % ch)
+            res[ch] = r
+        out_v = out.rearrange("(m p) t -> p m t", p=P)
+
+        def gelu(group, m):
+            ch, c0, c1 = GROUPS[group]
+            nc.scalar.activation(out=res[ch][:, m, c0:c1], in_=acc[(group, m)][:], func=GELU, bias=bias[:, m:m + 1])
+
+        def store(group, m0, m1):
+            ch, c0, c1 = GROUPS[group]
+            nc.sync.dma_start(
+                out=out_v[:, m0:m1, ch * CHUNK + c0:ch * CHUNK + c1], in_=res[ch][:, m0:m1, c0:c1])
+
+        V, S = nc.vector.tensor_copy, nc.scalar.copy
+
+        mask(0, 0, 2)
+        mask(0, 2, 4)
+        hi_copy(S, 0, 0)
+        hi_copy(S, 0, 1)
+        lo_sub(0, 0)
+        lo_sub(0, 1)
+        w_quant(0, 0)
+        warm_up(4)
+        nc.tensor.transpose(bT[:, 0:P], b_rows[:], ident[:])
+        x_copy(S, 0, 0, HALF, CHUNK)
+        x_copy(V, 0, 0, 0, HALF)
+        w_quant(0, 1)
+        mask(1, 0, 4, 0, HALF)
+        x_quant(0, 0)
+        for m in range(M_TILES):
+            matmuls(0, 0, m)
+        trunc_copy(1)
+        hi_copy(S, 1, 0)
+        lo_sub(1, 0)
+        x_copy(S, 1, 0, HALF, CHUNK)
+        x_copy(V, 1, 0, 0, HALF)
+        w_quant(1, 0)
+        nc.scalar.copy(out=bias[:], in_=bT[:, 0:M_TILES])
+        x_quant(1, 0)
+        for m in range(M_TILES):
+            matmuls(1, 0, m)
+        mask_pairs(1)
+        x_copy(S, 0, 1, HALF, CHUNK)
+        x_copy(V, 0, 1, 0, HALF)
+        lo_sub_packed(1)
+        x_quant(0, 1)
+        matmuls(0, 1, 0)
+        matmuls(0, 1, 1)
+        w_quant(1, 1)
+        matmuls(0, 1, 2)
+        matmuls(0, 1, 3)
+        x_copy(S, 1, 1, HALF, CHUNK)
+        x_copy(V, 1, 1, 0, HALF)
+        x_quant(1, 1)
+        for m in range(M_TILES):
+            matmuls(1, 1, m)
+        for m in range(M_TILES):
+            gelu(0, m)
+        store(0, 0, 2)
+        store(0, 2, 4)
+        x_copy(V, 2, 0)
+        x_quant(2, 0)
+        for m in range(M_TILES):
+            matmuls(2, 0, m)
+        gelu(1, 0)
+        gelu(1, 1)
+        store(1, 0, 2)
+        gelu(1, 2)
+        x_copy(V, 2, 1, 0, HALF)
+        x_copy(S, 2, 1, HALF + P, CHUNK)
+        x_copy(V, 2, 1, HALF, HALF + P)
+        x_quant(2, 1, 0, HALF)
+        gelu(1, 3)
+        store(1, 2, 4)
+        x_quant(2, 1, HALF, CHUNK)
+        for m in range(M_TILES):
+            matmuls(2, 1, m)
+            gelu(2, m)
+        store(2, 0, 4)
+        for m in range(M_TILES):
+            matmuls(3, 0, m)
+            matmuls(3, 1, m)
+            gelu(3, m)
+            if m == 1:
+                store(3, 0, 2)
+            if m > 1:
+                store(3, m, m + 1)

@@ -28,11 +28,11 @@ GELU = mybir.ActivationFunctionType.Gelu_apprx_tanh
 
 
 def rows_view(raw):
-    return raw.rearrange("p t (c i) -> p c t i", i=4)
+    return raw.rearrange("p t (c i) -> p c t i", i=2)
 
 
 def packed_view(grouped):
-    return grouped.rearrange("p (c i) t -> p c t i", i=4)
+    return grouped.rearrange("p (c i) t -> p c t i", i=2)
 
 
 def tile_mix_hilo_fm_gelu_kernel(tc, w, x, b, out):

@@ -10,8 +10,9 @@ K_PASS = P * PACK
 PASSES = K // K_PASS
 CHUNK = 512
 HALF = 256
+QUARTER = 128
 M_TILES = M // P
-GROUPS = [(0, 0, CHUNK), (1, 0, CHUNK), (2, 0, HALF), (2, HALF, CHUNK)]
+CHUNKS = T // CHUNK
 HI_MASK = -1048576
 HI_MASK_PAIR = -983056
 
@@ -37,7 +38,6 @@ def packed_view(grouped):
 
 def tile_mix_hilo_fm_gelu_kernel(tc, w, x, b, out):
     nc = tc.nc
-    chunks = T // CHUNK
 
     with ExitStack() as ctx:
         keep = ctx.enter_context(tc.tile_pool(name="keep", bufs=1))
@@ -45,38 +45,25 @@ def tile_mix_hilo_fm_gelu_kernel(tc, w, x, b, out):
         ctx.enter_context(tc.manual_schedule())
 
         w_raw = [keep.tile([P, PACK, M], F32, name="w_raw%d" % kp, align_bytes=64) for kp in range(PASSES)]
-        a_raw = [keep.tile([P, PACK, CHUNK], F32, name="a_raw%d" % kp, align_bytes=64) for kp in range(PASSES)]
-        b_raw = [keep.tile([P, PACK, CHUNK], F32, name="b_raw%d" % kp, align_bytes=64) for kp in range(PASSES)]
-        c_raw = [keep.tile([P, PACK, CHUNK], F32, name="c_raw%d" % kp, align_bytes=64) for kp in range(PASSES)]
-
-        def load_x(tile, kp, t0, t1):
-            nc.sync.dma_start(
-                out=tile[:],
-                in_=x[kp * K_PASS:(kp + 1) * K_PASS, t0:t1].rearrange("(p j) t -> p j t", j=PACK))
-
+        x_raw = {}
+        for ch in range(CHUNKS):
+            for kp in range(PASSES):
+                x_raw[(ch, kp)] = keep.tile([P, PACK, CHUNK], F32, name="x_raw%d_%d" % (ch, kp), align_bytes=64)
         w_rows = [w[kp * K_PASS:(kp + 1) * K_PASS, :].rearrange("(p j) c -> p j c", j=PACK) for kp in range(PASSES)]
-        nc.sync.dma_start(out=w_raw[0][:, 0:2, :], in_=w_rows[0][:, 0:2, :])
-        nc.sync.dma_start(out=w_raw[0][:, 2:4, :], in_=w_rows[0][:, 2:4, :])
-        load_x(a_raw[0], 0, 0, CHUNK)
-        nc.sync.dma_start(out=w_raw[1][:], in_=w_rows[1])
-        load_x(b_raw[0], 0, CHUNK, 2 * CHUNK)
-        load_x(a_raw[1], 1, 0, CHUNK)
-        load_x(b_raw[1], 1, CHUNK, 2 * CHUNK)
-        load_x(c_raw[0], 0, 2 * CHUNK, T)
-        load_x(c_raw[1], 1, 2 * CHUNK, T)
-        x_raw = {(ch, kp): tile[:] for kp in range(PASSES) for ch, tile in enumerate((a_raw[kp], b_raw[kp], c_raw[kp]))}
+
+        def load_w(kp, j0=0, j1=PACK):
+            nc.sync.dma_start(out=w_raw[kp][:, j0:j1, :], in_=w_rows[kp][:, j0:j1, :])
+
+        def load_x(ch, kp):
+            nc.sync.dma_start(
+                out=x_raw[(ch, kp)][:],
+                in_=x[kp * K_PASS:(kp + 1) * K_PASS, ch * CHUNK:(ch + 1) * CHUNK].rearrange("(p j) t -> p j t", j=PACK))
 
         warm = keep.tile([P, 1], F32, name="warm")
         warm_out = keep.tile([P, 1], F32, name="warm_out")
         b_rows = keep.tile([P, P], F32, name="b_rows")
         ident = keep.tile([P, P], F32, name="ident")
         bias = keep.tile([P, M_TILES], F32, name="bias")
-        nc.vector.memset(warm[:], 0.0)
-        nc.gpsimd.memset(b_rows[:], 0.0)
-        make_identity(nc, ident[:])
-        nc.scalar.dma_start(out=b_rows[0:M_TILES, :], in_=b.rearrange("(m p) -> m p", p=P))
-        nc.scalar.activation(out=warm_out[:], in_=warm[:], func=GELU)
-        bT = psum.tile([P, CHUNK], F32, name="bT", tag="acc7")
 
         hi_f = [keep.tile([P, PACK, M], F32, name="hi_f%d" % kp, align_bytes=64) for kp in range(PASSES)]
         w_grp = {}
@@ -84,58 +71,54 @@ def tile_mix_hilo_fm_gelu_kernel(tc, w, x, b, out):
         w_scales = {}
         for kp in range(PASSES):
             for h in range(2):
-                g = keep.tile([P, 2, HALF, PACK], BF16, name="w_grp%d_%d" % (kp, h), align_bytes=64)
-                c = keep.tile([P, 2, HALF], U32, name="w_codes%d_%d" % (kp, h), align_bytes=64)
-                s = keep.tile([P, 2, HALF], U8, name="w_scales%d_%d" % (kp, h), align_bytes=64)
-                w_grp[(kp, h)] = g
-                w_codes[(kp, h)] = c
-                w_scales[(kp, h)] = s
+                w_grp[(kp, h)] = keep.tile([P, 2, HALF, PACK], BF16, name="w_grp%d_%d" % (kp, h), align_bytes=64)
+                w_codes[(kp, h)] = keep.tile([P, 2, HALF], U32, name="w_codes%d_%d" % (kp, h), align_bytes=64)
+                w_scales[(kp, h)] = keep.tile([P, 2, HALF], U8, name="w_scales%d_%d" % (kp, h), align_bytes=64)
         x_grp = {}
         x_codes = {}
         x_scales = {}
-        for ch in range(chunks):
+        for ch in range(CHUNKS):
             for kp in range(PASSES):
-                g = keep.tile([P, CHUNK, PACK], BF16, name="x_grp%d_%d" % (ch, kp), align_bytes=64)
-                c = keep.tile([P, CHUNK], U32, name="x_codes%d_%d" % (ch, kp), align_bytes=64)
-                s = keep.tile([P, CHUNK], U8, name="x_scales%d_%d" % (ch, kp), align_bytes=64)
-                x_grp[(ch, kp)] = g
-                x_codes[(ch, kp)] = c
-                x_scales[(ch, kp)] = s
+                x_grp[(ch, kp)] = keep.tile([P, CHUNK, PACK], BF16, name="x_grp%d_%d" % (ch, kp), align_bytes=64)
+                x_codes[(ch, kp)] = keep.tile([P, CHUNK], U32, name="x_codes%d_%d" % (ch, kp), align_bytes=64)
+                x_scales[(ch, kp)] = keep.tile([P, CHUNK], U8, name="x_scales%d_%d" % (ch, kp), align_bytes=64)
+        res = [keep.tile([P, M_TILES, CHUNK], F32, name="res%d" % ch) for ch in range(CHUNKS)]
+        out_v = out.rearrange("(m p) t -> p m t", p=P)
 
         def mask(kp, j0, j1, c0=0, c1=M):
             nc.vector.tensor_scalar(
                 out=hi_f[kp][:, j0:j1, c0:c1].bitcast(I32), in0=w_raw[kp][:, j0:j1, c0:c1].bitcast(I32),
                 scalar1=HI_MASK, scalar2=None, op0=ALU.bitwise_and)
 
-        def hi_copy(copier, kp, h):
+        def hi_copy(kp, h):
             cols = slice(h * HALF, (h + 1) * HALF)
-            copier(out=packed_view(w_grp[(kp, h)][:, 0, :, :]), in_=rows_view(hi_f[kp][:, :, cols]))
+            nc.scalar.copy(out=packed_view(w_grp[(kp, h)][:, 0, :, :]), in_=rows_view(hi_f[kp][:, :, cols]))
 
-        def lo_sub(kp, h):
-            cols = slice(h * HALF, (h + 1) * HALF)
+        def lo_sub(kp, h, c0=0, c1=HALF):
+            cols = slice(h * HALF + c0, h * HALF + c1)
             nc.vector.tensor_tensor(
-                out=packed_view(w_grp[(kp, h)][:, 1, :, :]), in0=rows_view(w_raw[kp][:, :, cols]),
+                out=packed_view(w_grp[(kp, h)][:, 1, c0:c1, :]), in0=rows_view(w_raw[kp][:, :, cols]),
                 in1=rows_view(hi_f[kp][:, :, cols]), op=ALU.subtract)
 
-        def trunc_copy(h):
-            top = w_raw[1][:].bitcast(BF16)[:, :, 2 * h * HALF + 1:2 * (h + 1) * HALF:2]
-            nc.scalar.copy(out=packed_view(w_grp[(1, h)][:, 0, :, :]), in_=rows_view(top))
+        def trunc_copy(kp, h):
+            top = w_raw[kp][:].bitcast(BF16)[:, :, 2 * h * HALF + 1:2 * (h + 1) * HALF:2]
+            nc.scalar.copy(out=packed_view(w_grp[(kp, h)][:, 0, :, :]), in_=rows_view(top))
 
-        def mask_pairs(h):
-            words = w_grp[(1, h)][:, 0, :, :].rearrange("p c t -> p (c t)").bitcast(I32)
+        def mask_pairs(kp, h):
+            words = w_grp[(kp, h)][:, 0, :, :].rearrange("p c t -> p (c t)").bitcast(I32)
             nc.vector.tensor_scalar(out=words, in0=words, scalar1=HI_MASK_PAIR, scalar2=None, op0=ALU.bitwise_and)
 
-        def lo_sub_packed(h):
-            cols = slice(h * HALF, (h + 1) * HALF)
+        def lo_sub_packed(kp, h, c0=0, c1=HALF):
+            cols = slice(h * HALF + c0, h * HALF + c1)
             nc.vector.tensor_tensor(
-                out=packed_view(w_grp[(1, h)][:, 1, :, :]), in0=rows_view(w_raw[1][:, :, cols]),
-                in1=packed_view(w_grp[(1, h)][:, 0, :, :]), op=ALU.subtract)
+                out=packed_view(w_grp[(kp, h)][:, 1, c0:c1, :]), in0=rows_view(w_raw[kp][:, :, cols]),
+                in1=packed_view(w_grp[(kp, h)][:, 0, c0:c1, :]), op=ALU.subtract)
 
-        def w_quant(kp, h):
+        def w_quant(kp, h, s0=0, s1=2):
             nc.vector.quantize_mx(
-                out=w_codes[(kp, h)][:].rearrange("p s c -> p (s c)").bitcast(FP8X4),
-                scales=w_scales[(kp, h)][:].rearrange("p s c -> p (s c)"),
-                in_=w_grp[(kp, h)][:].rearrange("p s c t -> p (s c t)"))
+                out=w_codes[(kp, h)][:, s0:s1, :].rearrange("p s c -> p (s c)").bitcast(FP8X4),
+                scales=w_scales[(kp, h)][:, s0:s1, :].rearrange("p s c -> p (s c)"),
+                in_=w_grp[(kp, h)][:, s0:s1, :, :].rearrange("p s c t -> p (s c t)"))
 
         def x_copy(copier, ch, kp, c0=0, c1=CHUNK):
             copier(out=packed_view(x_grp[(ch, kp)][:, c0:c1, :]), in_=rows_view(x_raw[(ch, kp)][:, :, c0:c1]))
@@ -145,8 +128,8 @@ def tile_mix_hilo_fm_gelu_kernel(tc, w, x, b, out):
                 out=x_codes[(ch, kp)][:, c0:c1].bitcast(FP8X4), scales=x_scales[(ch, kp)][:, c0:c1],
                 in_=x_grp[(ch, kp)][:, c0:c1, :].rearrange("p c t -> p (c t)"))
 
-        def warm_up(passes):
-            scratch = psum.tile([P, CHUNK], F32, name="scratch", tag="acc6")
+        def warm_up(passes, bank):
+            scratch = psum.tile([P, CHUNK], F32, name="scratch", tag="bank%d" % bank)
             for i in range(passes):
                 nc.tensor.matmul_mx(
                     out=scratch[:],
@@ -158,108 +141,138 @@ def tile_mix_hilo_fm_gelu_kernel(tc, w, x, b, out):
 
         acc = {}
 
-        def matmuls(group, kp, m):
-            ch, c0, c1 = GROUPS[group]
-            if kp == 0:
-                a = psum.tile([P, c1 - c0], F32, name="acc%d_%d" % (group, m), tag="acc%d" % ((group % 2) * M_TILES + m))
-                acc[(group, m)] = a
+        def open_acc(ch, m, bank, g0=0, g1=CHUNK):
+            acc[(ch, m, g0)] = psum.tile([P, g1 - g0], F32, name="acc%d_%d_%d" % (ch, m, g0), tag="bank%d" % bank)
+
+        def mm(ch, kp, m, c0=0, c1=CHUNK, g0=0, first=False, last=False, parts=(0, 1)):
             h = m // 2
-            for part in range(2):
-                cols = slice((m % 2) * P, (m % 2 + 1) * P)
+            cols = slice((m % 2) * P, (m % 2 + 1) * P)
+            for part in parts:
                 nc.tensor.matmul_mx(
-                    out=acc[(group, m)][:],
+                    out=acc[(ch, m, g0)][:, c0 - g0:c1 - g0],
                     lhsT=w_codes[(kp, h)][:, part, cols].bitcast(FP8X4),
                     lhsT_scale=w_scales[(kp, h)][:, part, cols],
                     rhs=x_codes[(ch, kp)][:, c0:c1].bitcast(FP8X4),
                     rhs_scale=x_scales[(ch, kp)][:, c0:c1],
-                    start=(kp == 0 and part == 0), stop=(kp == PASSES - 1 and part == 1))
+                    start=(first and part == parts[0]), stop=(last and part == parts[-1]))
 
-        res = {}
-        for ch in range(chunks):
-            r = keep.tile([P, M_TILES, CHUNK], F32, name="res%d" % ch)
-            res[ch] = r
-        out_v = out.rearrange("(m p) t -> p m t", p=P)
+        def gelu(ch, m, g0=0, g1=CHUNK):
+            nc.scalar.activation(out=res[ch][:, m, g0:g1], in_=acc[(ch, m, g0)][:], func=GELU, bias=bias[:, m:m + 1])
 
-        def gelu(group, m):
-            ch, c0, c1 = GROUPS[group]
-            nc.scalar.activation(out=res[ch][:, m, c0:c1], in_=acc[(group, m)][:], func=GELU, bias=bias[:, m:m + 1])
+        def store(ch, m0, m1, c0=0, c1=CHUNK, queue=nc.sync):
+            queue.dma_start(out=out_v[:, m0:m1, ch * CHUNK + c0:ch * CHUNK + c1], in_=res[ch][:, m0:m1, c0:c1])
 
-        def store(group, m0, m1):
-            ch, c0, c1 = GROUPS[group]
-            nc.sync.dma_start(
-                out=out_v[:, m0:m1, ch * CHUNK + c0:ch * CHUNK + c1], in_=res[ch][:, m0:m1, c0:c1])
+        def bias_load(queue):
+            nc.vector.memset(b_rows[:], 0.0)
+            nc.vector.memset(warm[:], 0.0)
+            make_identity(nc, ident[:])
+            queue.dma_start(out=b_rows[0:M_TILES, :], in_=b.rearrange("(m p) -> m p", p=P))
+            nc.scalar.activation(out=warm_out[:], in_=warm[:], func=GELU)
+
+        def bias_turn(bank):
+            turned = psum.tile([P, P], F32, name="turned", tag="bank%d" % bank)
+            nc.tensor.transpose(turned[:], b_rows[:], ident[:])
+            return turned
 
         V, S = nc.vector.tensor_copy, nc.scalar.copy
+        A, B, C = 0, 1, 2
 
-        mask(0, 0, 2)
-        mask(0, 2, 4)
-        hi_copy(S, 0, 0)
-        hi_copy(S, 0, 1)
+        load_w(0, 0, 3)
+        bias_load(nc.sync)
+        load_w(0, 3, 4)
+        load_x(A, 0)
+        load_w(1)
+        load_x(B, 0)
+        load_x(A, 1)
+        load_x(B, 1)
+        load_x(C, 0)
+        load_x(C, 1)
+        turned = bias_turn(7)
+
+        mask(0, 0, 3)
+        mask(0, 3, 4, 0, HALF)
+        mask(0, 3, 4, HALF, M)
+        hi_copy(0, 0)
+        hi_copy(0, 1)
         lo_sub(0, 0)
         lo_sub(0, 1)
         w_quant(0, 0)
-        warm_up(4)
-        nc.tensor.transpose(bT[:, 0:P], b_rows[:], ident[:])
-        x_copy(S, 0, 0, HALF, CHUNK)
-        x_copy(V, 0, 0, 0, HALF)
+        warm_up(4, 6)
+        x_copy(S, A, 0, QUARTER, CHUNK)
+        x_copy(V, A, 0, 0, QUARTER)
         w_quant(0, 1)
+        V(out=bias[:], in_=turned[:, 0:M_TILES])
         mask(1, 0, 4, 0, HALF)
-        x_quant(0, 0)
+        x_quant(A, 0)
         for m in range(M_TILES):
-            matmuls(0, 0, m)
-        trunc_copy(1)
-        hi_copy(S, 1, 0)
+            open_acc(A, m, m)
+            mm(A, 0, m, first=True)
+        trunc_copy(1, 1)
+        hi_copy(1, 0)
         lo_sub(1, 0)
-        x_copy(S, 1, 0, HALF, CHUNK)
-        x_copy(V, 1, 0, 0, HALF)
+        mask_pairs(1, 1)
         w_quant(1, 0)
-        nc.scalar.copy(out=bias[:], in_=bT[:, 0:M_TILES])
-        x_quant(1, 0)
+        x_copy(S, B, 0, 0, HALF)
+        x_copy(S, B, 0, HALF, CHUNK)
+        lo_sub_packed(1, 1, 0, QUARTER)
+        x_quant(B, 0, 0, HALF)
         for m in range(M_TILES):
-            matmuls(1, 0, m)
-        mask_pairs(1)
-        x_copy(S, 0, 1, HALF, CHUNK)
-        x_copy(V, 0, 1, 0, HALF)
-        lo_sub_packed(1)
-        x_quant(0, 1)
-        matmuls(0, 1, 0)
-        matmuls(0, 1, 1)
-        w_quant(1, 1)
-        matmuls(0, 1, 2)
-        matmuls(0, 1, 3)
-        x_copy(S, 1, 1, HALF, CHUNK)
-        x_copy(V, 1, 1, 0, HALF)
-        x_quant(1, 1)
+            open_acc(B, m, M_TILES + m)
+            mm(B, 0, m, 0, HALF, first=True)
+        lo_sub_packed(1, 1, QUARTER, HALF)
+        x_quant(B, 0, HALF, CHUNK)
         for m in range(M_TILES):
-            matmuls(1, 1, m)
+            mm(B, 0, m, HALF, CHUNK)
+        x_copy(S, A, 1, HALF, CHUNK)
+        x_copy(V, A, 1, 0, HALF)
+        w_quant(1, 1, 0, 1)
+        x_quant(A, 1, 0, HALF)
+        x_quant(A, 1, HALF, CHUNK)
+        for m in range(2):
+            mm(A, 1, m, 0, HALF)
+        for m in range(2):
+            mm(A, 1, m, HALF, CHUNK, last=True)
+        x_copy(S, B, 1, 320, CHUNK)
+        x_copy(V, B, 1, 0, 320)
+        w_quant(1, 1, 1, 2)
+        for m in range(2, M_TILES):
+            mm(A, 1, m, last=True)
+        x_quant(B, 1)
         for m in range(M_TILES):
-            gelu(0, m)
-        store(0, 0, 2)
-        store(0, 2, 4)
-        x_copy(V, 2, 0)
-        x_quant(2, 0)
+            mm(B, 1, m, last=True)
         for m in range(M_TILES):
-            matmuls(2, 0, m)
-        gelu(1, 0)
-        gelu(1, 1)
-        store(1, 0, 2)
-        gelu(1, 2)
-        x_copy(V, 2, 1, 0, HALF)
-        x_copy(S, 2, 1, HALF + P, CHUNK)
-        x_copy(V, 2, 1, HALF, HALF + P)
-        x_quant(2, 1, 0, HALF)
-        gelu(1, 3)
-        store(1, 2, 4)
-        x_quant(2, 1, HALF, CHUNK)
-        for m in range(M_TILES):
-            matmuls(2, 1, m)
-            gelu(2, m)
-        store(2, 0, 4)
-        for m in range(M_TILES):
-            matmuls(3, 0, m)
-            matmuls(3, 1, m)
-            gelu(3, m)
+            gelu(A, m)
+            if m % 2 == 1:
+                store(A, m - 1, m + 1)
+        x_copy(V, C, 0, 0, HALF)
+        x_copy(V, C, 0, HALF, CHUNK)
+        x_quant(C, 0, 0, HALF)
+        x_quant(C, 0, HALF, CHUNK)
+        for m in range(3):
+            open_acc(C, m, m)
+            mm(C, 0, m, first=True)
+        for m in range(3):
+            gelu(B, m)
             if m == 1:
-                store(3, 0, 2)
-            if m > 1:
-                store(3, m, m + 1)
+                store(B, 0, 2)
+        x_copy(S, C, 1, HALF + QUARTER, CHUNK)
+        gelu(B, 3)
+        store(B, 2, 4)
+        x_copy(V, C, 1, 0, HALF)
+        x_copy(V, C, 1, HALF, HALF + QUARTER)
+        x_quant(C, 1, 0, HALF)
+        x_quant(C, 1, HALF, CHUNK)
+        mm(C, 1, 0, 0, HALF)
+        mm(C, 1, 0, HALF, CHUNK, last=True)
+        gelu(C, 0)
+        store(C, 0, 1)
+        for m in range(1, 3):
+            mm(C, 1, m, last=True)
+            gelu(C, m)
+            store(C, m, m + 1)
+        for g0 in (0, HALF):
+            open_acc(C, 3, 3 + g0 // HALF, g0, g0 + HALF)
+            mm(C, 0, 3, g0, g0 + HALF, g0, first=True)
+            mm(C, 1, 3, g0, g0 + HALF, g0, last=True)
+            gelu(C, 3, g0, g0 + HALF)
+            store(C, 3, 4, g0, g0 + HALF)

@@ -44,11 +44,11 @@ def tile_mix_hilo_fm_gelu_kernel(tc, w, x, b, out):
         psum = ctx.enter_context(tc.psum_pool(name="psum", bufs=1))
         ctx.enter_context(tc.manual_schedule())
 
-        w_raw = [keep.tile([P, PACK, M], F32, name="w_raw%d" % kp, align_bytes=64) for kp in range(PASSES)]
+        w_raw = [keep.tile([P, PACK, M], F32, name="w_raw%d" % kp, align_bytes=256) for kp in range(PASSES)]
         x_raw = {}
         for ch in range(CHUNKS):
             for kp in range(PASSES):
-                x_raw[(ch, kp)] = keep.tile([P, PACK, CHUNK], F32, name="x_raw%d_%d" % (ch, kp), align_bytes=64)
+                x_raw[(ch, kp)] = keep.tile([P, PACK, CHUNK], F32, name="x_raw%d_%d" % (ch, kp), align_bytes=256)
         w_rows = [w[kp * K_PASS:(kp + 1) * K_PASS, :].rearrange("(p j) c -> p j c", j=PACK) for kp in range(PASSES)]
 
         def load_w(kp, j0=0, j1=PACK):
@@ -82,7 +82,7 @@ def tile_mix_hilo_fm_gelu_kernel(tc, w, x, b, out):
                 x_grp[(ch, kp)] = keep.tile([P, CHUNK, PACK], BF16, name="x_grp%d_%d" % (ch, kp), align_bytes=64)
                 x_codes[(ch, kp)] = keep.tile([P, CHUNK], U32, name="x_codes%d_%d" % (ch, kp), align_bytes=64)
                 x_scales[(ch, kp)] = keep.tile([P, CHUNK], U8, name="x_scales%d_%d" % (ch, kp), align_bytes=64)
-        res = [keep.tile([P, M_TILES, CHUNK], F32, name="res%d" % ch) for ch in range(CHUNKS)]
+        res = [keep.tile([P, M_TILES, CHUNK], F32, name="res%d" % ch, align_bytes=256) for ch in range(CHUNKS)]
         out_v = out.rearrange("(m p) t -> p m t", p=P)
 
         def mask(kp, j0, j1, c0=0, c1=M):

@@ -29,11 +29,11 @@ GELU = mybir.ActivationFunctionType.Gelu_apprx_tanh
 
 
 def rows_view(raw):
-    return raw.rearrange("p t (c i) -> p c t i", i=2)
+    return raw.rearrange("p t (c i) -> p c t i", i=4)
 
 
 def packed_view(grouped):
-    return grouped.rearrange("p (c i) t -> p c t i", i=2)
+    return grouped.rearrange("p (c i) t -> p c t i", i=4)
 
 
 def tile_mix_hilo_fm_gelu_kernel(tc, w, x, b, out):

@@ -6,8 +6,8 @@ from concourse.masks import make_identity
 K, M, T = 1024, 512, 1536
 P = 128
 PACK = 4
-K_PASS = P * PACK
-PASSES = K // K_PASS
+K_SLAB = P * PACK
+SLABS = K // K_SLAB
 CHUNK = 512
 HALF = 256
 QUARTER = 128
@@ -15,6 +15,7 @@ M_TILES = M // P
 CHUNKS = T // CHUNK
 HI_MASK = -1048576
 HI_MASK_PAIR = -983056
+HI, LO = 0, 1
 
 FLOPS = 2 * 2 * K * M * T
 
@@ -44,89 +45,90 @@ def tile_mix_hilo_fm_gelu_kernel(tc, w, x, b, out):
         psum = ctx.enter_context(tc.psum_pool(name="psum", bufs=1))
         ctx.enter_context(tc.manual_schedule())
 
-        w_raw = [keep.tile([P, PACK, M], F32, name="w_raw%d" % kp, align_bytes=256) for kp in range(PASSES)]
+        w_raw = [keep.tile([P, PACK, M], F32, name="w_raw%d" % s, align_bytes=256) for s in range(SLABS)]
         x_raw = {}
         for ch in range(CHUNKS):
-            for kp in range(PASSES):
-                x_raw[(ch, kp)] = keep.tile([P, PACK, CHUNK], F32, name="x_raw%d_%d" % (ch, kp), align_bytes=256)
-        w_rows = [w[kp * K_PASS:(kp + 1) * K_PASS, :].rearrange("(p j) c -> p j c", j=PACK) for kp in range(PASSES)]
-
-        def load_w(kp, j0=0, j1=PACK):
-            nc.sync.dma_start(out=w_raw[kp][:, j0:j1, :], in_=w_rows[kp][:, j0:j1, :])
-
-        def load_x(ch, kp):
-            nc.sync.dma_start(
-                out=x_raw[(ch, kp)][:],
-                in_=x[kp * K_PASS:(kp + 1) * K_PASS, ch * CHUNK:(ch + 1) * CHUNK].rearrange("(p j) t -> p j t", j=PACK))
-
-        warm = keep.tile([P, 1], F32, name="warm")
-        warm_out = keep.tile([P, 1], F32, name="warm_out")
-        b_rows = keep.tile([P, P], F32, name="b_rows")
-        ident = keep.tile([P, P], F32, name="ident")
-        bias = keep.tile([P, M_TILES], F32, name="bias")
-
-        hi_f = [keep.tile([P, PACK, M], F32, name="hi_f%d" % kp, align_bytes=64) for kp in range(PASSES)]
+            for s in range(SLABS):
+                x_raw[(ch, s)] = keep.tile([P, PACK, CHUNK], F32, name="x_raw%d_%d" % (ch, s), align_bytes=256)
+        res = [keep.tile([P, M_TILES, CHUNK], F32, name="res%d" % ch, align_bytes=256) for ch in range(CHUNKS)]
+        hi_f = [keep.tile([P, PACK, M], F32, name="hi_f%d" % s, align_bytes=256) for s in range(SLABS)]
         w_grp = {}
         w_codes = {}
         w_scales = {}
-        for kp in range(PASSES):
+        for s in range(SLABS):
             for h in range(2):
-                w_grp[(kp, h)] = keep.tile([P, 2, HALF, PACK], BF16, name="w_grp%d_%d" % (kp, h), align_bytes=64)
-                w_codes[(kp, h)] = keep.tile([P, 2, HALF], U32, name="w_codes%d_%d" % (kp, h), align_bytes=64)
-                w_scales[(kp, h)] = keep.tile([P, 2, HALF], U8, name="w_scales%d_%d" % (kp, h), align_bytes=64)
+                w_grp[(s, h)] = keep.tile([P, 2, HALF, PACK], BF16, name="w_grp%d_%d" % (s, h), align_bytes=64)
+                w_codes[(s, h)] = keep.tile([P, 2, HALF], U32, name="w_codes%d_%d" % (s, h), align_bytes=64)
+                w_scales[(s, h)] = keep.tile([P, 2, HALF], U8, name="w_scales%d_%d" % (s, h), align_bytes=64)
         x_grp = {}
         x_codes = {}
         x_scales = {}
         for ch in range(CHUNKS):
-            for kp in range(PASSES):
-                x_grp[(ch, kp)] = keep.tile([P, CHUNK, PACK], BF16, name="x_grp%d_%d" % (ch, kp), align_bytes=64)
-                x_codes[(ch, kp)] = keep.tile([P, CHUNK], U32, name="x_codes%d_%d" % (ch, kp), align_bytes=64)
-                x_scales[(ch, kp)] = keep.tile([P, CHUNK], U8, name="x_scales%d_%d" % (ch, kp), align_bytes=64)
-        res = [keep.tile([P, M_TILES, CHUNK], F32, name="res%d" % ch, align_bytes=256) for ch in range(CHUNKS)]
+            for s in range(SLABS):
+                x_grp[(ch, s)] = keep.tile([P, CHUNK, PACK], BF16, name="x_grp%d_%d" % (ch, s), align_bytes=64)
+                x_codes[(ch, s)] = keep.tile([P, CHUNK], U32, name="x_codes%d_%d" % (ch, s), align_bytes=64)
+                x_scales[(ch, s)] = keep.tile([P, CHUNK], U8, name="x_scales%d_%d" % (ch, s), align_bytes=64)
+        b_rows = keep.tile([P, P], F32, name="b_rows", align_bytes=256)
+        ident = keep.tile([P, P], F32, name="ident")
+        bias = keep.tile([P, M_TILES], F32, name="bias")
+        warm = keep.tile([P, 1], F32, name="warm")
+        warm_out = keep.tile([P, 1], F32, name="warm_out")
         out_v = out.rearrange("(m p) t -> p m t", p=P)
 
-        def mask(kp, j0, j1, c0=0, c1=M):
+        def load_w(s, j0=0, j1=PACK):
+            rows = w[s * K_SLAB:(s + 1) * K_SLAB, :].rearrange("(p j) c -> p j c", j=PACK)
+            nc.sync.dma_start(out=w_raw[s][:, j0:j1, :], in_=rows[:, j0:j1, :])
+
+        def load_x(ch, s):
+            nc.sync.dma_start(
+                out=x_raw[(ch, s)][:],
+                in_=x[s * K_SLAB:(s + 1) * K_SLAB, ch * CHUNK:(ch + 1) * CHUNK].rearrange("(p j) t -> p j t", j=PACK))
+
+        def load_bias():
+            nc.sync.dma_start(out=b_rows[0:M_TILES, :], in_=b.rearrange("(m p) -> m p", p=P))
+
+        def mask(s, j0, j1, c0, c1):
             nc.vector.tensor_scalar(
-                out=hi_f[kp][:, j0:j1, c0:c1].bitcast(I32), in0=w_raw[kp][:, j0:j1, c0:c1].bitcast(I32),
+                out=hi_f[s][:, j0:j1, c0:c1].bitcast(I32), in0=w_raw[s][:, j0:j1, c0:c1].bitcast(I32),
                 scalar1=HI_MASK, scalar2=None, op0=ALU.bitwise_and)
 
-        def hi_copy(kp, h):
-            cols = slice(h * HALF, (h + 1) * HALF)
-            nc.scalar.copy(out=packed_view(w_grp[(kp, h)][:, 0, :, :]), in_=rows_view(hi_f[kp][:, :, cols]))
+        def hi_copy(s, h, c0=0, c1=HALF):
+            cols = slice(h * HALF + c0, h * HALF + c1)
+            nc.scalar.copy(out=packed_view(w_grp[(s, h)][:, HI, c0:c1, :]), in_=rows_view(hi_f[s][:, :, cols]))
 
-        def lo_sub(kp, h, c0=0, c1=HALF):
+        def lo_sub(s, h, c0=0, c1=HALF):
             cols = slice(h * HALF + c0, h * HALF + c1)
             nc.vector.tensor_tensor(
-                out=packed_view(w_grp[(kp, h)][:, 1, c0:c1, :]), in0=rows_view(w_raw[kp][:, :, cols]),
-                in1=rows_view(hi_f[kp][:, :, cols]), op=ALU.subtract)
+                out=packed_view(w_grp[(s, h)][:, LO, c0:c1, :]), in0=rows_view(w_raw[s][:, :, cols]),
+                in1=rows_view(hi_f[s][:, :, cols]), op=ALU.subtract)
 
-        def trunc_copy(kp, h):
-            top = w_raw[kp][:].bitcast(BF16)[:, :, 2 * h * HALF + 1:2 * (h + 1) * HALF:2]
-            nc.scalar.copy(out=packed_view(w_grp[(kp, h)][:, 0, :, :]), in_=rows_view(top))
+        def top_copy(copier, s, h, c0=0, c1=HALF):
+            top = w_raw[s][:].bitcast(BF16)[:, :, 2 * (h * HALF + c0) + 1:2 * (h * HALF + c1):2]
+            copier(out=packed_view(w_grp[(s, h)][:, HI, c0:c1, :]), in_=rows_view(top))
 
-        def mask_pairs(kp, h):
-            words = w_grp[(kp, h)][:, 0, :, :].rearrange("p c t -> p (c t)").bitcast(I32)
+        def mask_pairs(s, h, c0=0, c1=HALF):
+            words = w_grp[(s, h)][:, HI, c0:c1, :].rearrange("p c t -> p (c t)").bitcast(I32)
             nc.vector.tensor_scalar(out=words, in0=words, scalar1=HI_MASK_PAIR, scalar2=None, op0=ALU.bitwise_and)
 
-        def lo_sub_packed(kp, h, c0=0, c1=HALF):
+        def lo_sub_packed(s, h, c0=0, c1=HALF):
             cols = slice(h * HALF + c0, h * HALF + c1)
             nc.vector.tensor_tensor(
-                out=packed_view(w_grp[(kp, h)][:, 1, c0:c1, :]), in0=rows_view(w_raw[kp][:, :, cols]),
-                in1=packed_view(w_grp[(kp, h)][:, 0, c0:c1, :]), op=ALU.subtract)
+                out=packed_view(w_grp[(s, h)][:, LO, c0:c1, :]), in0=rows_view(w_raw[s][:, :, cols]),
+                in1=packed_view(w_grp[(s, h)][:, HI, c0:c1, :]), op=ALU.subtract)
 
-        def w_quant(kp, h, s0=0, s1=2):
+        def w_quant(s, h, part0=HI, part1=LO + 1, c0=0, c1=HALF):
             nc.vector.quantize_mx(
-                out=w_codes[(kp, h)][:, s0:s1, :].rearrange("p s c -> p (s c)").bitcast(FP8X4),
-                scales=w_scales[(kp, h)][:, s0:s1, :].rearrange("p s c -> p (s c)"),
-                in_=w_grp[(kp, h)][:, s0:s1, :, :].rearrange("p s c t -> p (s c t)"))
+                out=w_codes[(s, h)][:, part0:part1, c0:c1].rearrange("p s c -> p (s c)").bitcast(FP8X4),
+                scales=w_scales[(s, h)][:, part0:part1, c0:c1].rearrange("p s c -> p (s c)"),
+                in_=w_grp[(s, h)][:, part0:part1, c0:c1, :].rearrange("p s c t -> p (s c t)"))
 
-        def x_copy(copier, ch, kp, c0=0, c1=CHUNK):
-            copier(out=packed_view(x_grp[(ch, kp)][:, c0:c1, :]), in_=rows_view(x_raw[(ch, kp)][:, :, c0:c1]))
+        def x_copy(copier, ch, s, c0=0, c1=CHUNK):
+            copier(out=packed_view(x_grp[(ch, s)][:, c0:c1, :]), in_=rows_view(x_raw[(ch, s)][:, :, c0:c1]))
 
-        def x_quant(ch, kp, c0=0, c1=CHUNK):
+        def x_quant(ch, s, c0=0, c1=CHUNK):
             nc.vector.quantize_mx(
-                out=x_codes[(ch, kp)][:, c0:c1].bitcast(FP8X4), scales=x_scales[(ch, kp)][:, c0:c1],
-                in_=x_grp[(ch, kp)][:, c0:c1, :].rearrange("p c t -> p (c t)"))
+                out=x_codes[(ch, s)][:, c0:c1].bitcast(FP8X4), scales=x_scales[(ch, s)][:, c0:c1],
+                in_=x_grp[(ch, s)][:, c0:c1, :].rearrange("p c t -> p (c t)"))
 
         def warm_up(passes, bank):
             scratch = psum.tile([P, CHUNK], F32, name="scratch", tag="bank%d" % bank)
@@ -144,42 +146,35 @@ def tile_mix_hilo_fm_gelu_kernel(tc, w, x, b, out):
         def open_acc(ch, m, bank, g0=0, g1=CHUNK):
             acc[(ch, m, g0)] = psum.tile([P, g1 - g0], F32, name="acc%d_%d_%d" % (ch, m, g0), tag="bank%d" % bank)
 
-        def mm(ch, kp, m, c0=0, c1=CHUNK, g0=0, first=False, last=False, parts=(0, 1)):
+        def mm(ch, s, m, c0=0, c1=CHUNK, g0=0, first=False, last=False, parts=(HI, LO)):
             h = m // 2
             cols = slice((m % 2) * P, (m % 2 + 1) * P)
             for part in parts:
                 nc.tensor.matmul_mx(
                     out=acc[(ch, m, g0)][:, c0 - g0:c1 - g0],
-                    lhsT=w_codes[(kp, h)][:, part, cols].bitcast(FP8X4),
-                    lhsT_scale=w_scales[(kp, h)][:, part, cols],
-                    rhs=x_codes[(ch, kp)][:, c0:c1].bitcast(FP8X4),
-                    rhs_scale=x_scales[(ch, kp)][:, c0:c1],
+                    lhsT=w_codes[(s, h)][:, part, cols].bitcast(FP8X4),
+                    lhsT_scale=w_scales[(s, h)][:, part, cols],
+                    rhs=x_codes[(ch, s)][:, c0:c1].bitcast(FP8X4),
+                    rhs_scale=x_scales[(ch, s)][:, c0:c1],
                     start=(first and part == parts[0]), stop=(last and part == parts[-1]))
 
         def gelu(ch, m, g0=0, g1=CHUNK):
             nc.scalar.activation(out=res[ch][:, m, g0:g1], in_=acc[(ch, m, g0)][:], func=GELU, bias=bias[:, m:m + 1])
 
-        def store(ch, m0, m1, c0=0, c1=CHUNK, queue=nc.sync):
-            queue.dma_start(out=out_v[:, m0:m1, ch * CHUNK + c0:ch * CHUNK + c1], in_=res[ch][:, m0:m1, c0:c1])
-
-        def bias_load(queue):
-            nc.vector.memset(b_rows[:], 0.0)
-            nc.vector.memset(warm[:], 0.0)
-            make_identity(nc, ident[:])
-            queue.dma_start(out=b_rows[0:M_TILES, :], in_=b.rearrange("(m p) -> m p", p=P))
-            nc.scalar.activation(out=warm_out[:], in_=warm[:], func=GELU)
-
-        def bias_turn(bank):
-            turned = psum.tile([P, P], F32, name="turned", tag="bank%d" % bank)
-            nc.tensor.transpose(turned[:], b_rows[:], ident[:])
-            return turned
+        def store(ch, m0, m1, c0=0, c1=CHUNK):
+            nc.sync.dma_start(out=out_v[:, m0:m1, ch * CHUNK + c0:ch * CHUNK + c1], in_=res[ch][:, m0:m1, c0:c1])
 
         V, S = nc.vector.tensor_copy, nc.scalar.copy
         A, B, C = 0, 1, 2
 
+        nc.vector.memset(b_rows[:], 0.0)
+        nc.vector.memset(warm[:], 0.0)
+        make_identity(nc, ident[:])
+        nc.scalar.activation(out=warm_out[:], in_=warm[:], func=GELU)
+
         load_w(0, 0, 3)
-        bias_load(nc.sync)
         load_w(0, 3, 4)
+        load_bias()
         load_x(A, 0)
         load_w(1)
         load_x(B, 0)
@@ -187,92 +182,103 @@ def tile_mix_hilo_fm_gelu_kernel(tc, w, x, b, out):
         load_x(B, 1)
         load_x(C, 0)
         load_x(C, 1)
-        turned = bias_turn(7)
+        turned = psum.tile([P, P], F32, name="turned", tag="bank7")
+        nc.tensor.transpose(turned[:], b_rows[:], ident[:])
 
-        mask(0, 0, 3)
+        mask(0, 0, 3, 0, HALF)
         mask(0, 3, 4, 0, HALF)
-        mask(0, 3, 4, HALF, M)
+        top_copy(S, 0, 1)
         hi_copy(0, 0)
-        hi_copy(0, 1)
         lo_sub(0, 0)
-        lo_sub(0, 1)
-        w_quant(0, 0)
+        mask_pairs(0, 1)
+        w_quant(0, 0, LO, LO + 1)
+        lo_sub_packed(0, 1)
+        w_quant(0, 0, HI, HI + 1)
         warm_up(4, 6)
-        x_copy(S, A, 0, QUARTER, CHUNK)
-        x_copy(V, A, 0, 0, QUARTER)
         w_quant(0, 1)
+        x_copy(S, A, 0, 0, HALF)
+        x_copy(S, A, 0, HALF, CHUNK)
+        x_quant(A, 0, 0, HALF)
         V(out=bias[:], in_=turned[:, 0:M_TILES])
-        mask(1, 0, 4, 0, HALF)
-        x_quant(A, 0)
         for m in range(M_TILES):
             open_acc(A, m, m)
-            mm(A, 0, m, first=True)
-        trunc_copy(1, 1)
+            mm(A, 0, m, 0, HALF, first=True)
+        mask(1, 0, 4, 0, HALF)
+        x_quant(A, 0, HALF, CHUNK)
+        for m in range(M_TILES):
+            mm(A, 0, m, HALF, CHUNK)
+        top_copy(S, 1, 1)
         hi_copy(1, 0)
         lo_sub(1, 0)
         mask_pairs(1, 1)
-        w_quant(1, 0)
-        x_copy(S, B, 0, 0, HALF)
+        x_copy(S, B, 0, 176, HALF)
+        x_copy(V, B, 0, 0, 176)
         x_copy(S, B, 0, HALF, CHUNK)
-        lo_sub_packed(1, 1, 0, QUARTER)
+        w_quant(1, 0, HI, HI + 1)
         x_quant(B, 0, 0, HALF)
         for m in range(M_TILES):
             open_acc(B, m, M_TILES + m)
             mm(B, 0, m, 0, HALF, first=True)
-        lo_sub_packed(1, 1, QUARTER, HALF)
+        w_quant(1, 0, LO, LO + 1)
+        lo_sub_packed(1, 1, 0, QUARTER)
         x_quant(B, 0, HALF, CHUNK)
         for m in range(M_TILES):
             mm(B, 0, m, HALF, CHUNK)
+        x_copy(S, A, 1, 176, HALF)
         x_copy(S, A, 1, HALF, CHUNK)
-        x_copy(V, A, 1, 0, HALF)
-        w_quant(1, 1, 0, 1)
+        x_copy(V, A, 1, 0, 176)
+        w_quant(1, 1, HI, HI + 1)
         x_quant(A, 1, 0, HALF)
-        x_quant(A, 1, HALF, CHUNK)
-        for m in range(2):
+        lo_sub_packed(1, 1, QUARTER, HALF)
+        w_quant(1, 1, LO, LO + 1, 0, QUARTER)
+        for m in range(3):
             mm(A, 1, m, 0, HALF)
-        for m in range(2):
+        mm(A, 1, 3, 0, HALF, parts=(HI,))
+        x_quant(A, 1, HALF, CHUNK)
+        w_quant(1, 1, LO, LO + 1, QUARTER, HALF)
+        for m in range(3):
             mm(A, 1, m, HALF, CHUNK, last=True)
-        x_copy(S, B, 1, 320, CHUNK)
-        x_copy(V, B, 1, 0, 320)
-        w_quant(1, 1, 1, 2)
-        for m in range(2, M_TILES):
-            mm(A, 1, m, last=True)
-        x_quant(B, 1)
-        for m in range(M_TILES):
+        mm(A, 1, 3, HALF, CHUNK, parts=(HI,))
+        mm(A, 1, 3, last=True, parts=(LO,))
+        x_copy(S, B, 1, 400, CHUNK)
+        x_copy(V, B, 1, 0, HALF)
+        x_copy(V, B, 1, HALF, 400)
+        x_quant(B, 1, 0, HALF)
+        x_quant(B, 1, HALF, CHUNK)
+        mm(B, 1, 0, 0, HALF)
+        mm(B, 1, 0, HALF, CHUNK, last=True)
+        for m in range(1, M_TILES):
             mm(B, 1, m, last=True)
         for m in range(M_TILES):
             gelu(A, m)
             if m % 2 == 1:
                 store(A, m - 1, m + 1)
         x_copy(V, C, 0, 0, HALF)
-        x_copy(V, C, 0, HALF, CHUNK)
+        x_copy(V, C, 0, HALF, HALF + QUARTER)
         x_quant(C, 0, 0, HALF)
+        x_copy(V, C, 0, HALF + QUARTER, CHUNK)
+        for m in range(M_TILES):
+            open_acc(C, m, m, 0, HALF)
+            mm(C, 0, m, 0, HALF, first=True)
         x_quant(C, 0, HALF, CHUNK)
         for m in range(3):
-            open_acc(C, m, m)
-            mm(C, 0, m, first=True)
-        for m in range(3):
             gelu(B, m)
-            if m == 1:
-                store(B, 0, 2)
-        x_copy(S, C, 1, HALF + QUARTER, CHUNK)
-        gelu(B, 3)
-        store(B, 2, 4)
+        store(B, 0, 3)
+        for m in range(3):
+            open_acc(C, m, M_TILES + m, HALF, CHUNK)
+            mm(C, 0, m, HALF, CHUNK, HALF, first=True)
+        x_copy(S, C, 1, 384, CHUNK)
         x_copy(V, C, 1, 0, HALF)
-        x_copy(V, C, 1, HALF, HALF + QUARTER)
+        x_copy(V, C, 1, HALF, 384)
+        gelu(B, 3)
+        store(B, 3, 4)
         x_quant(C, 1, 0, HALF)
         x_quant(C, 1, HALF, CHUNK)
-        mm(C, 1, 0, 0, HALF)
-        mm(C, 1, 0, HALF, CHUNK, last=True)
-        gelu(C, 0)
-        store(C, 0, 1)
-        for m in range(1, 3):
-            mm(C, 1, m, last=True)
-            gelu(C, m)
+        for m in range(M_TILES):
+            for g0 in (0, HALF):
+                if m == 3 and g0 == HALF:
+                    open_acc(C, m, M_TILES + m, HALF, CHUNK)
+                    mm(C, 0, m, HALF, CHUNK, HALF, first=True)
+                mm(C, 1, m, g0, g0 + HALF, g0, last=True)
+                gelu(C, m, g0, g0 + HALF)
             store(C, m, m + 1)
-        for g0 in (0, HALF):
-            open_acc(C, 3, 3 + g0 // HALF, g0, g0 + HALF)
-            mm(C, 0, 3, g0, g0 + HALF, g0, first=True)
-            mm(C, 1, 3, g0, g0 + HALF, g0, last=True)
-            gelu(C, 3, g0, g0 + HALF)
-            store(C, 3, 4, g0, g0 + HALF)

@@ -45,13 +45,21 @@ def tile_mix_hilo_fm_gelu_kernel(tc, w, x, b, out):
         psum = ctx.enter_context(tc.psum_pool(name="psum", bufs=1))
         ctx.enter_context(tc.manual_schedule())
 
-        w_raw = [keep.tile([P, PACK, M], F32, name="w_raw%d" % s, align_bytes=256) for s in range(SLABS)]
+        w_first = [keep.tile([P, PACK, HALF], F32, name="w_first%d" % h, align_bytes=256) for h in range(2)]
+        w_second = keep.tile([P, PACK, M], F32, name="w_second", align_bytes=256)
+        w_raw = {(0, 0): w_first[0][:], (0, 1): w_first[1][:],
+                 (1, 0): w_second[:, :, 0:HALF], (1, 1): w_second[:, :, HALF:M]}
+        w_top = {(0, 0): w_first[0][:].bitcast(BF16), (0, 1): w_first[1][:].bitcast(BF16),
+                 (1, 0): w_second[:].bitcast(BF16)[:, :, 0:M], (1, 1): w_second[:].bitcast(BF16)[:, :, M:2 * M]}
         x_raw = {}
         for ch in range(CHUNKS):
             for s in range(SLABS):
                 x_raw[(ch, s)] = keep.tile([P, PACK, CHUNK], F32, name="x_raw%d_%d" % (ch, s), align_bytes=256)
         res = [keep.tile([P, M_TILES, CHUNK], F32, name="res%d" % ch, align_bytes=256) for ch in range(CHUNKS)]
-        hi_f = [keep.tile([P, PACK, M], F32, name="hi_f%d" % s, align_bytes=256) for s in range(SLABS)]
+        hi_f = {}
+        for s in range(SLABS):
+            for h in range(2):
+                hi_f[(s, h)] = keep.tile([P, PACK, HALF], F32, name="hi_f%d_%d" % (s, h), align_bytes=256)
         w_grp = {}
         w_codes = {}
         w_scales = {}
@@ -75,9 +83,8 @@ def tile_mix_hilo_fm_gelu_kernel(tc, w, x, b, out):
         warm_out = keep.tile([P, 1], F32, name="warm_out")
         out_v = out.rearrange("(m p) t -> p m t", p=P)
 
-        def load_w(s, j0=0, j1=PACK):
-            rows = w[s * K_SLAB:(s + 1) * K_SLAB, :].rearrange("(p j) c -> p j c", j=PACK)
-            nc.sync.dma_start(out=w_raw[s][:, j0:j1, :], in_=rows[:, j0:j1, :])
+        def w_rows(s):
+            return w[s * K_SLAB:(s + 1) * K_SLAB, :].rearrange("(p j) c -> p j c", j=PACK)
 
         def load_x(ch, s):
             nc.sync.dma_start(
@@ -87,23 +94,21 @@ def tile_mix_hilo_fm_gelu_kernel(tc, w, x, b, out):
         def load_bias():
             nc.sync.dma_start(out=b_rows[0:M_TILES, :], in_=b.rearrange("(m p) -> m p", p=P))
 
-        def mask(s, j0, j1, c0, c1):
+        def mask(s, h, c0=0, c1=HALF):
             nc.vector.tensor_scalar(
-                out=hi_f[s][:, j0:j1, c0:c1].bitcast(I32), in0=w_raw[s][:, j0:j1, c0:c1].bitcast(I32),
+                out=hi_f[(s, h)][:, :, c0:c1].bitcast(I32), in0=w_raw[(s, h)][:, :, c0:c1].bitcast(I32),
                 scalar1=HI_MASK, scalar2=None, op0=ALU.bitwise_and)
 
         def hi_copy(s, h, c0=0, c1=HALF):
-            cols = slice(h * HALF + c0, h * HALF + c1)
-            nc.scalar.copy(out=packed_view(w_grp[(s, h)][:, HI, c0:c1, :]), in_=rows_view(hi_f[s][:, :, cols]))
+            nc.scalar.copy(out=packed_view(w_grp[(s, h)][:, HI, c0:c1, :]), in_=rows_view(hi_f[(s, h)][:, :, c0:c1]))
 
         def lo_sub(s, h, c0=0, c1=HALF):
-            cols = slice(h * HALF + c0, h * HALF + c1)
             nc.vector.tensor_tensor(
-                out=packed_view(w_grp[(s, h)][:, LO, c0:c1, :]), in0=rows_view(w_raw[s][:, :, cols]),
-                in1=rows_view(hi_f[s][:, :, cols]), op=ALU.subtract)
+                out=packed_view(w_grp[(s, h)][:, LO, c0:c1, :]), in0=rows_view(w_raw[(s, h)][:, :, c0:c1]),
+                in1=rows_view(hi_f[(s, h)][:, :, c0:c1]), op=ALU.subtract)
 
         def top_copy(copier, s, h, c0=0, c1=HALF):
-            top = w_raw[s][:].bitcast(BF16)[:, :, 2 * (h * HALF + c0) + 1:2 * (h * HALF + c1):2]
+            top = w_top[(s, h)][:, :, 2 * c0 + 1:2 * c1:2]
             copier(out=packed_view(w_grp[(s, h)][:, HI, c0:c1, :]), in_=rows_view(top))
 
         def mask_pairs(s, h, c0=0, c1=HALF):
@@ -111,9 +116,8 @@ def tile_mix_hilo_fm_gelu_kernel(tc, w, x, b, out):
             nc.vector.tensor_scalar(out=words, in0=words, scalar1=HI_MASK_PAIR, scalar2=None, op0=ALU.bitwise_and)
 
         def lo_sub_packed(s, h, c0=0, c1=HALF):
-            cols = slice(h * HALF + c0, h * HALF + c1)
             nc.vector.tensor_tensor(
-                out=packed_view(w_grp[(s, h)][:, LO, c0:c1, :]), in0=rows_view(w_raw[s][:, :, cols]),
+                out=packed_view(w_grp[(s, h)][:, LO, c0:c1, :]), in0=rows_view(w_raw[(s, h)][:, :, c0:c1]),
                 in1=packed_view(w_grp[(s, h)][:, HI, c0:c1, :]), op=ALU.subtract)
 
         def w_quant(s, h, part0=HI, part1=LO + 1, c0=0, c1=HALF):
@@ -172,11 +176,11 @@ def tile_mix_hilo_fm_gelu_kernel(tc, w, x, b, out):
         make_identity(nc, ident[:])
         nc.scalar.activation(out=warm_out[:], in_=warm[:], func=GELU)
 
-        load_w(0, 0, 3)
-        load_w(0, 3, 4)
+        nc.sync.dma_start(out=w_first[0][:], in_=w_rows(0)[:, :, 0:HALF])
+        nc.sync.dma_start(out=w_first[1][:], in_=w_rows(0)[:, :, HALF:M])
         load_bias()
         load_x(A, 0)
-        load_w(1)
+        nc.sync.dma_start(out=w_second[:], in_=w_rows(1))
         load_x(B, 0)
         load_x(A, 1)
         load_x(B, 1)
@@ -185,64 +189,61 @@ def tile_mix_hilo_fm_gelu_kernel(tc, w, x, b, out):
         turned = psum.tile([P, P], F32, name="turned", tag="bank7")
         nc.tensor.transpose(turned[:], b_rows[:], ident[:])
 
-        mask(0, 0, 3, 0, HALF)
-        mask(0, 3, 4, 0, HALF)
-        top_copy(S, 0, 1)
-        hi_copy(0, 0)
-        lo_sub(0, 0)
-        mask_pairs(0, 1)
-        w_quant(0, 0, LO, LO + 1)
-        lo_sub_packed(0, 1)
-        w_quant(0, 0, HI, HI + 1)
+        mask(0, 0, 0, QUARTER)
+        mask(0, 0, QUARTER, HALF)
+        hi_copy(0, 0, 0, QUARTER)
+        hi_copy(0, 0, QUARTER, HALF)
+        lo_sub(0, 0, 0, QUARTER)
+        lo_sub(0, 0, QUARTER, HALF)
+        mask(0, 1)
+        hi_copy(0, 1)
+        w_quant(0, 0)
         warm_up(4, 6)
-        w_quant(0, 1)
-        x_copy(S, A, 0, 0, HALF)
+        lo_sub(0, 1)
         x_copy(S, A, 0, HALF, CHUNK)
-        x_quant(A, 0, 0, HALF)
-        V(out=bias[:], in_=turned[:, 0:M_TILES])
+        x_copy(V, A, 0, 0, HALF)
+        w_quant(0, 1, HI, HI + 1)
+        w_quant(0, 1, LO, LO + 1)
+        x_quant(A, 0)
         for m in range(M_TILES):
             open_acc(A, m, m)
-            mm(A, 0, m, 0, HALF, first=True)
-        mask(1, 0, 4, 0, HALF)
-        x_quant(A, 0, HALF, CHUNK)
-        for m in range(M_TILES):
-            mm(A, 0, m, HALF, CHUNK)
-        top_copy(S, 1, 1)
+            mm(A, 0, m, first=True)
+        V(out=bias[:], in_=turned[:, 0:M_TILES])
+        mask(1, 0)
+        mask(1, 1)
         hi_copy(1, 0)
+        hi_copy(1, 1, 0, 64)
         lo_sub(1, 0)
-        mask_pairs(1, 1)
         x_copy(S, B, 0, 176, HALF)
-        x_copy(V, B, 0, 0, 176)
         x_copy(S, B, 0, HALF, CHUNK)
+        hi_copy(1, 1, 64, HALF)
+        x_copy(V, B, 0, 0, 176)
         w_quant(1, 0, HI, HI + 1)
         x_quant(B, 0, 0, HALF)
         for m in range(M_TILES):
             open_acc(B, m, M_TILES + m)
             mm(B, 0, m, 0, HALF, first=True)
         w_quant(1, 0, LO, LO + 1)
-        lo_sub_packed(1, 1, 0, QUARTER)
+        lo_sub(1, 1, 0, QUARTER)
         x_quant(B, 0, HALF, CHUNK)
         for m in range(M_TILES):
             mm(B, 0, m, HALF, CHUNK)
-        x_copy(S, A, 1, 176, HALF)
         x_copy(S, A, 1, HALF, CHUNK)
-        x_copy(V, A, 1, 0, 176)
-        w_quant(1, 1, HI, HI + 1)
+        x_copy(V, A, 1, 0, HALF)
+        lo_sub(1, 1, QUARTER, 192)
         x_quant(A, 1, 0, HALF)
-        lo_sub_packed(1, 1, QUARTER, HALF)
-        w_quant(1, 1, LO, LO + 1, 0, QUARTER)
-        for m in range(3):
-            mm(A, 1, m, 0, HALF)
-        mm(A, 1, 3, 0, HALF, parts=(HI,))
+        lo_sub(1, 1, 192, HALF)
         x_quant(A, 1, HALF, CHUNK)
-        w_quant(1, 1, LO, LO + 1, QUARTER, HALF)
-        for m in range(3):
+        w_quant(1, 1)
+        for m in range(2):
+            mm(A, 1, m, 0, HALF)
+        for m in range(2):
             mm(A, 1, m, HALF, CHUNK, last=True)
-        mm(A, 1, 3, HALF, CHUNK, parts=(HI,))
-        mm(A, 1, 3, last=True, parts=(LO,))
-        x_copy(S, B, 1, 400, CHUNK)
+        for m in range(2, M_TILES):
+            mm(A, 1, m, last=True)
+        x_copy(S, B, 1, 448, CHUNK)
         x_copy(V, B, 1, 0, HALF)
-        x_copy(V, B, 1, HALF, 400)
+        x_copy(V, B, 1, HALF, 448)
         x_quant(B, 1, 0, HALF)
         x_quant(B, 1, HALF, CHUNK)
         mm(B, 1, 0, 0, HALF)
@@ -251,34 +252,37 @@ def tile_mix_hilo_fm_gelu_kernel(tc, w, x, b, out):
             mm(B, 1, m, last=True)
         for m in range(M_TILES):
             gelu(A, m)
-            if m % 2 == 1:
-                store(A, m - 1, m + 1)
+        store(A, 0, 4)
         x_copy(V, C, 0, 0, HALF)
         x_copy(V, C, 0, HALF, HALF + QUARTER)
         x_quant(C, 0, 0, HALF)
         x_copy(V, C, 0, HALF + QUARTER, CHUNK)
-        for m in range(M_TILES):
-            open_acc(C, m, m, 0, HALF)
+        open_acc(C, 0, 0, 0, HALF)
+        mm(C, 0, 0, 0, HALF, first=True)
+        for m in range(1, 3):
+            open_acc(C, m, m)
             mm(C, 0, m, 0, HALF, first=True)
         x_quant(C, 0, HALF, CHUNK)
-        for m in range(3):
+        gelu(B, 0)
+        for m in range(1, 3):
+            mm(C, 0, m, HALF, CHUNK)
+        open_acc(C, 0, M_TILES, HALF, CHUNK)
+        mm(C, 0, 0, HALF, CHUNK, HALF, first=True)
+        open_acc(C, 3, 3)
+        mm(C, 0, 3, first=True)
+        for m in range(1, M_TILES):
             gelu(B, m)
-        store(B, 0, 3)
-        for m in range(3):
-            open_acc(C, m, M_TILES + m, HALF, CHUNK)
-            mm(C, 0, m, HALF, CHUNK, HALF, first=True)
-        x_copy(S, C, 1, 384, CHUNK)
+        store(B, 0, 4)
+        x_copy(S, C, 1, 416, CHUNK)
         x_copy(V, C, 1, 0, HALF)
-        x_copy(V, C, 1, HALF, 384)
-        gelu(B, 3)
-        store(B, 3, 4)
+        x_copy(V, C, 1, HALF, 416)
         x_quant(C, 1, 0, HALF)
         x_quant(C, 1, HALF, CHUNK)
-        for m in range(M_TILES):
-            for g0 in (0, HALF):
-                if m == 3 and g0 == HALF:
-                    open_acc(C, m, M_TILES + m, HALF, CHUNK)
-                    mm(C, 0, m, HALF, CHUNK, HALF, first=True)
-                mm(C, 1, m, g0, g0 + HALF, g0, last=True)
-                gelu(C, m, g0, g0 + HALF)
+        for g0 in (0, HALF):
+            mm(C, 1, 0, g0, g0 + HALF, g0, last=True)
+            gelu(C, 0, g0, g0 + HALF)
+        store(C, 0, 1)
+        for m in range(1, M_TILES):
+            mm(C, 1, m, last=True)
+            gelu(C, m)
             store(C, m, m + 1)

@@ -252,37 +252,37 @@ def tile_mix_hilo_fm_gelu_kernel(tc, w, x, b, out):
             mm(B, 1, m, last=True)
         for m in range(M_TILES):
             gelu(A, m)
-        store(A, 0, 4)
+            if m % 2 == 1:
+                store(A, m - 1, m + 1)
         x_copy(V, C, 0, 0, HALF)
-        x_copy(V, C, 0, HALF, HALF + QUARTER)
+        x_copy(V, C, 0, HALF, CHUNK)
         x_quant(C, 0, 0, HALF)
-        x_copy(V, C, 0, HALF + QUARTER, CHUNK)
-        open_acc(C, 0, 0, 0, HALF)
-        mm(C, 0, 0, 0, HALF, first=True)
-        for m in range(1, 3):
-            open_acc(C, m, m)
-            mm(C, 0, m, 0, HALF, first=True)
         x_quant(C, 0, HALF, CHUNK)
-        gelu(B, 0)
-        for m in range(1, 3):
-            mm(C, 0, m, HALF, CHUNK)
-        open_acc(C, 0, M_TILES, HALF, CHUNK)
-        mm(C, 0, 0, HALF, CHUNK, HALF, first=True)
-        open_acc(C, 3, 3)
-        mm(C, 0, 3, first=True)
-        for m in range(1, M_TILES):
+        for m in range(3):
+            open_acc(C, m, m)
+            mm(C, 0, m, first=True)
+        for m in range(3):
             gelu(B, m)
-        store(B, 0, 4)
-        x_copy(S, C, 1, 416, CHUNK)
+            if m == 1:
+                store(B, 0, 2)
+        x_copy(S, C, 1, HALF + QUARTER, CHUNK)
+        gelu(B, 3)
+        store(B, 2, 4)
         x_copy(V, C, 1, 0, HALF)
-        x_copy(V, C, 1, HALF, 416)
+        x_copy(V, C, 1, HALF, HALF + QUARTER)
         x_quant(C, 1, 0, HALF)
         x_quant(C, 1, HALF, CHUNK)
-        for g0 in (0, HALF):
-            mm(C, 1, 0, g0, g0 + HALF, g0, last=True)
-            gelu(C, 0, g0, g0 + HALF)
+        mm(C, 1, 0, 0, HALF)
+        mm(C, 1, 0, HALF, CHUNK, last=True)
+        gelu(C, 0)
         store(C, 0, 1)
-        for m in range(1, M_TILES):
+        for m in range(1, 3):
             mm(C, 1, m, last=True)
             gelu(C, m)
             store(C, m, m + 1)
+        for g0 in (0, HALF):
+            open_acc(C, 3, 3 + g0 // HALF, g0, g0 + HALF)
+            mm(C, 0, 3, g0, g0 + HALF, g0, first=True)
+            mm(C, 1, 3, g0, g0 + HALF, g0, last=True)
+            gelu(C, 3, g0, g0 + HALF)
+            store(C, 3, 4, g0, g0 + HALF)

@@ -177,8 +177,8 @@ def tile_mix_hilo_fm_gelu_kernel(tc, w, x, b, out):
         nc.scalar.activation(out=warm_out[:], in_=warm[:], func=GELU)
 
         nc.sync.dma_start(out=w_first[0][:], in_=w_rows(0)[:, :, 0:HALF])
-        nc.sync.dma_start(out=w_first[1][:], in_=w_rows(0)[:, :, HALF:M])
         load_bias()
+        nc.sync.dma_start(out=w_first[1][:], in_=w_rows(0)[:, :, HALF:M])
         load_x(A, 0)
         nc.sync.dma_start(out=w_second[:], in_=w_rows(1))
         load_x(B, 0)
@@ -197,53 +197,44 @@ def tile_mix_hilo_fm_gelu_kernel(tc, w, x, b, out):
         lo_sub(0, 0, QUARTER, HALF)
         mask(0, 1)
         hi_copy(0, 1)
-        w_quant(0, 0)
-        warm_up(4, 6)
+        w_quant(0, 0, LO, LO + 1)
         lo_sub(0, 1)
-        x_copy(S, A, 0, HALF, CHUNK)
-        x_copy(V, A, 0, 0, HALF)
-        w_quant(0, 1, HI, HI + 1)
-        w_quant(0, 1, LO, LO + 1)
+        w_quant(0, 0, HI, HI + 1)
+        x_copy(S, A, 0, 256, CHUNK)
+        x_copy(V, A, 0, 0, 256)
+        w_quant(0, 1)
         x_quant(A, 0)
         for m in range(M_TILES):
             open_acc(A, m, m)
             mm(A, 0, m, first=True)
+        warm_up(1, 6)
         V(out=bias[:], in_=turned[:, 0:M_TILES])
         mask(1, 0)
         mask(1, 1)
         hi_copy(1, 0)
-        hi_copy(1, 1, 0, 64)
         lo_sub(1, 0)
-        x_copy(S, B, 0, 176, HALF)
-        x_copy(S, B, 0, HALF, CHUNK)
-        hi_copy(1, 1, 64, HALF)
-        x_copy(V, B, 0, 0, 176)
-        w_quant(1, 0, HI, HI + 1)
-        x_quant(B, 0, 0, HALF)
+        x_copy(S, B, 0, 320, CHUNK)
+        x_copy(V, B, 0, 0, 320)
+        w_quant(1, 0, LO, LO + 1)
+        x_quant(B, 0)
         for m in range(M_TILES):
             open_acc(B, m, M_TILES + m)
-            mm(B, 0, m, 0, HALF, first=True)
-        w_quant(1, 0, LO, LO + 1)
+            mm(B, 0, m, first=True)
+        hi_copy(1, 1)
         lo_sub(1, 1, 0, QUARTER)
-        x_quant(B, 0, HALF, CHUNK)
+        x_copy(S, A, 1, 320, CHUNK)
+        x_copy(V, A, 1, 0, 320)
+        w_quant(1, 0, HI, HI + 1)
+        x_quant(A, 1)
+        lo_sub(1, 1, QUARTER, HALF)
+        w_quant(1, 1, HI, HI + 1)
+        x_copy(V, B, 1, 0, QUARTER)
+        w_quant(1, 1, LO, LO + 1)
         for m in range(M_TILES):
-            mm(B, 0, m, HALF, CHUNK)
-        x_copy(S, A, 1, HALF, CHUNK)
-        x_copy(V, A, 1, 0, HALF)
-        lo_sub(1, 1, QUARTER, 192)
-        x_quant(A, 1, 0, HALF)
-        lo_sub(1, 1, 192, HALF)
-        x_quant(A, 1, HALF, CHUNK)
-        w_quant(1, 1)
-        for m in range(2):
-            mm(A, 1, m, 0, HALF)
-        for m in range(2):
-            mm(A, 1, m, HALF, CHUNK, last=True)
-        for m in range(2, M_TILES):
             mm(A, 1, m, last=True)
-        x_copy(S, B, 1, 448, CHUNK)
-        x_copy(V, B, 1, 0, HALF)
-        x_copy(V, B, 1, HALF, 448)
+        x_copy(S, B, 1, 320, CHUNK)
+        x_copy(V, B, 1, QUARTER, HALF)
+        x_copy(V, B, 1, HALF, 320)
         x_quant(B, 1, 0, HALF)
         x_quant(B, 1, HALF, CHUNK)
         mm(B, 1, 0, 0, HALF)

from contextlib import ExitStack

import concourse.mybir as mybir
from concourse.masks import make_identity

K, M, T = 1024, 512, 1536
P = 128
PACK = 4
K_SLAB = P * PACK
SLABS = K // K_SLAB
CHUNK = 512
HALF = 256
QUARTER = 128
M_TILES = M // P
CHUNKS = T // CHUNK
HI_MASK = -1048576
HI_MASK_PAIR = -983056
HI, LO = 0, 1

FLOPS = 2 * 2 * K * M * T

F32 = mybir.dt.float32
BF16 = mybir.dt.bfloat16
I32 = mybir.dt.int32
U32 = mybir.dt.uint32
U8 = mybir.dt.uint8
FP8X4 = mybir.dt.float8_e4m3fn_x4
ALU = mybir.AluOpType
GELU = mybir.ActivationFunctionType.Gelu_apprx_tanh


def rows_view(raw):
    return raw.rearrange("p t (c i) -> p c t i", i=4)


def packed_view(grouped):
    return grouped.rearrange("p (c i) t -> p c t i", i=4)


def tile_mix_hilo_fm_gelu_kernel(tc, w, x, b, out):
    nc = tc.nc

    with ExitStack() as ctx:
        keep = ctx.enter_context(tc.tile_pool(name="keep", bufs=1))
        psum = ctx.enter_context(tc.psum_pool(name="psum", bufs=1))
        ctx.enter_context(tc.manual_schedule())

        w_first = [keep.tile([P, PACK, HALF], F32, name="w_first%d" % h, align_bytes=256) for h in range(2)]
        w_second = keep.tile([P, PACK, M], F32, name="w_second", align_bytes=256)
        w_raw = {(0, 0): w_first[0][:], (0, 1): w_first[1][:],
                 (1, 0): w_second[:, :, 0:HALF], (1, 1): w_second[:, :, HALF:M]}
        w_top = {(0, 0): w_first[0][:].bitcast(BF16), (0, 1): w_first[1][:].bitcast(BF16),
                 (1, 0): w_second[:].bitcast(BF16)[:, :, 0:M], (1, 1): w_second[:].bitcast(BF16)[:, :, M:2 * M]}
        x_raw = {}
        for ch in range(CHUNKS):
            for s in range(SLABS):
                x_raw[(ch, s)] = keep.tile([P, PACK, CHUNK], F32, name="x_raw%d_%d" % (ch, s), align_bytes=256)
        res = [keep.tile([P, M_TILES, CHUNK], F32, name="res%d" % ch, align_bytes=256) for ch in range(CHUNKS)]
        hi_f = {}
        for s in range(SLABS):
            for h in range(2):
                hi_f[(s, h)] = keep.tile([P, PACK, HALF], F32, name="hi_f%d_%d" % (s, h), align_bytes=256)
        w_grp = {}
        w_codes = {}
        w_scales = {}
        for s in range(SLABS):
            for h in range(2):
                w_grp[(s, h)] = keep.tile([P, 2, HALF, PACK], BF16, name="w_grp%d_%d" % (s, h), align_bytes=64)
                w_codes[(s, h)] = keep.tile([P, 2, HALF], U32, name="w_codes%d_%d" % (s, h), align_bytes=64)
                w_scales[(s, h)] = keep.tile([P, 2, HALF], U8, name="w_scales%d_%d" % (s, h), align_bytes=64)
        x_grp = {}
        x_codes = {}
        x_scales = {}
        for ch in range(CHUNKS):
            for s in range(SLABS):
                x_grp[(ch, s)] = keep.tile([P, CHUNK, PACK], BF16, name="x_grp%d_%d" % (ch, s), align_bytes=64)
                x_codes[(ch, s)] = keep.tile([P, CHUNK], U32, name="x_codes%d_%d" % (ch, s), align_bytes=64)
                x_scales[(ch, s)] = keep.tile([P, CHUNK], U8, name="x_scales%d_%d" % (ch, s), align_bytes=64)
        b_rows = keep.tile([P, P], F32, name="b_rows", align_bytes=256)
        ident = keep.tile([P, P], F32, name="ident")
        bias = keep.tile([P, M_TILES], F32, name="bias")
        warm = keep.tile([P, 1], F32, name="warm")
        warm_out = keep.tile([P, 1], F32, name="warm_out")
        out_v = out.rearrange("(m p) t -> p m t", p=P)

        def w_rows(s):
            return w[s * K_SLAB:(s + 1) * K_SLAB, :].rearrange("(p j) c -> p j c", j=PACK)

        def load_x(ch, s):
            nc.sync.dma_start(
                out=x_raw[(ch, s)][:],
                in_=x[s * K_SLAB:(s + 1) * K_SLAB, ch * CHUNK:(ch + 1) * CHUNK].rearrange("(p j) t -> p j t", j=PACK))

        def load_bias():
            nc.sync.dma_start(out=b_rows[0:M_TILES, :], in_=b.rearrange("(m p) -> m p", p=P))

        def mask(s, h, c0=0, c1=HALF):
            nc.vector.tensor_scalar(
                out=hi_f[(s, h)][:, :, c0:c1].bitcast(I32), in0=w_raw[(s, h)][:, :, c0:c1].bitcast(I32),
                scalar1=HI_MASK, scalar2=None, op0=ALU.bitwise_and)

        def hi_copy(s, h, c0=0, c1=HALF):
            nc.scalar.copy(out=packed_view(w_grp[(s, h)][:, HI, c0:c1, :]), in_=rows_view(hi_f[(s, h)][:, :, c0:c1]))

        def lo_sub(s, h, c0=0, c1=HALF):
            nc.vector.tensor_tensor(
                out=packed_view(w_grp[(s, h)][:, LO, c0:c1, :]), in0=rows_view(w_raw[(s, h)][:, :, c0:c1]),
                in1=rows_view(hi_f[(s, h)][:, :, c0:c1]), op=ALU.subtract)

        def top_copy(copier, s, h, c0=0, c1=HALF):
            top = w_top[(s, h)][:, :, 2 * c0 + 1:2 * c1:2]
            copier(out=packed_view(w_grp[(s, h)][:, HI, c0:c1, :]), in_=rows_view(top))

        def mask_pairs(s, h, c0=0, c1=HALF):
            words = w_grp[(s, h)][:, HI, c0:c1, :].rearrange("p c t -> p (c t)").bitcast(I32)
            nc.vector.tensor_scalar(out=words, in0=words, scalar1=HI_MASK_PAIR, scalar2=None, op0=ALU.bitwise_and)

        def lo_sub_packed(s, h, c0=0, c1=HALF):
            nc.vector.tensor_tensor(
                out=packed_view(w_grp[(s, h)][:, LO, c0:c1, :]), in0=rows_view(w_raw[(s, h)][:, :, c0:c1]),
                in1=packed_view(w_grp[(s, h)][:, HI, c0:c1, :]), op=ALU.subtract)

        def w_quant(s, h, part0=HI, part1=LO + 1, c0=0, c1=HALF):
            nc.vector.quantize_mx(
                out=w_codes[(s, h)][:, part0:part1, c0:c1].rearrange("p s c -> p (s c)").bitcast(FP8X4),
                scales=w_scales[(s, h)][:, part0:part1, c0:c1].rearrange("p s c -> p (s c)"),
                in_=w_grp[(s, h)][:, part0:part1, c0:c1, :].rearrange("p s c t -> p (s c t)"))

        def x_copy(copier, ch, s, c0=0, c1=CHUNK):
            copier(out=packed_view(x_grp[(ch, s)][:, c0:c1, :]), in_=rows_view(x_raw[(ch, s)][:, :, c0:c1]))

        def x_quant(ch, s, c0=0, c1=CHUNK):
            nc.vector.quantize_mx(
                out=x_codes[(ch, s)][:, c0:c1].bitcast(FP8X4), scales=x_scales[(ch, s)][:, c0:c1],
                in_=x_grp[(ch, s)][:, c0:c1, :].rearrange("p c t -> p (c t)"))

        def warm_up(passes, bank):
            scratch = psum.tile([P, CHUNK], F32, name="scratch", tag="bank%d" % bank)
            for i in range(passes):
                nc.tensor.matmul_mx(
                    out=scratch[:],
                    lhsT=w_codes[(0, 0)][:, 0, 0:P].bitcast(FP8X4),
                    lhsT_scale=w_scales[(0, 0)][:, 0, 0:P],
                    rhs=w_codes[(0, 0)][:].rearrange("p s c -> p (s c)").bitcast(FP8X4),
                    rhs_scale=w_scales[(0, 0)][:].rearrange("p s c -> p (s c)"),
                    start=True, stop=True)

        acc = {}

        def open_acc(ch, m, bank, g0=0, g1=CHUNK):
            acc[(ch, m, g0)] = psum.tile([P, g1 - g0], F32, name="acc%d_%d_%d" % (ch, m, g0), tag="bank%d" % bank)

        def mm(ch, s, m, c0=0, c1=CHUNK, g0=0, first=False, last=False, parts=(HI, LO)):
            h = m // 2
            cols = slice((m % 2) * P, (m % 2 + 1) * P)
            for part in parts:
                nc.tensor.matmul_mx(
                    out=acc[(ch, m, g0)][:, c0 - g0:c1 - g0],
                    lhsT=w_codes[(s, h)][:, part, cols].bitcast(FP8X4),
                    lhsT_scale=w_scales[(s, h)][:, part, cols],
                    rhs=x_codes[(ch, s)][:, c0:c1].bitcast(FP8X4),
                    rhs_scale=x_scales[(ch, s)][:, c0:c1],
                    start=(first and part == parts[0]), stop=(last and part == parts[-1]))

        def gelu(ch, m, g0=0, g1=CHUNK):
            nc.scalar.activation(out=res[ch][:, m, g0:g1], in_=acc[(ch, m, g0)][:], func=GELU, bias=bias[:, m:m + 1])

        def store(ch, m0, m1, c0=0, c1=CHUNK):
            nc.sync.dma_start(out=out_v[:, m0:m1, ch * CHUNK + c0:ch * CHUNK + c1], in_=res[ch][:, m0:m1, c0:c1])

        V, S = nc.vector.tensor_copy, nc.scalar.copy
        A, B, C = 0, 1, 2

        nc.vector.memset(b_rows[:], 0.0)
        nc.vector.memset(warm[:], 0.0)
        make_identity(nc, ident[:])
        nc.scalar.activation(out=warm_out[:], in_=warm[:], func=GELU)

        nc.sync.dma_start(out=w_first[0][:], in_=w_rows(0)[:, :, 0:HALF])
        load_bias()
        nc.sync.dma_start(out=w_first[1][:], in_=w_rows(0)[:, :, HALF:M])
        load_x(A, 0)
        nc.sync.dma_start(out=w_second[:], in_=w_rows(1))
        load_x(B, 0)
        load_x(A, 1)
        load_x(B, 1)
        load_x(C, 0)
        load_x(C, 1)
        turned = psum.tile([P, P], F32, name="turned", tag="bank7")
        nc.tensor.transpose(turned[:], b_rows[:], ident[:])

        mask(0, 0, 0, QUARTER)
        mask(0, 0, QUARTER, HALF)
        hi_copy(0, 0, 0, QUARTER)
        hi_copy(0, 0, QUARTER, HALF)
        lo_sub(0, 0, 0, QUARTER)
        lo_sub(0, 0, QUARTER, HALF)
        mask(0, 1)
        hi_copy(0, 1)
        w_quant(0, 0, LO, LO + 1)
        lo_sub(0, 1)
        w_quant(0, 0, HI, HI + 1)
        x_copy(S, A, 0, 256, CHUNK)
        x_copy(V, A, 0, 0, 256)
        w_quant(0, 1)
        x_quant(A, 0)
        for m in range(M_TILES):
            open_acc(A, m, m)
            mm(A, 0, m, first=True)
        warm_up(1, 6)
        V(out=bias[:], in_=turned[:, 0:M_TILES])
        mask(1, 0)
        mask(1, 1)
        hi_copy(1, 0)
        lo_sub(1, 0)
        x_copy(S, B, 0, 320, CHUNK)
        x_copy(V, B, 0, 0, 320)
        w_quant(1, 0, LO, LO + 1)
        x_quant(B, 0)
        for m in range(M_TILES):
            open_acc(B, m, M_TILES + m)
            mm(B, 0, m, first=True)
        hi_copy(1, 1)
        lo_sub(1, 1, 0, QUARTER)
        x_copy(S, A, 1, 320, CHUNK)
        x_copy(V, A, 1, 0, 320)
        w_quant(1, 0, HI, HI + 1)
        x_quant(A, 1)
        lo_sub(1, 1, QUARTER, HALF)
        w_quant(1, 1, HI, HI + 1)
        x_copy(V, B, 1, 0, QUARTER)
        w_quant(1, 1, LO, LO + 1)
        for m in range(M_TILES):
            mm(A, 1, m, last=True)
        x_copy(S, B, 1, 320, CHUNK)
        x_copy(V, B, 1, QUARTER, HALF)
        x_copy(V, B, 1, HALF, 320)
        x_quant(B, 1, 0, HALF)
        x_quant(B, 1, HALF, CHUNK)
        mm(B, 1, 0, 0, HALF)
        mm(B, 1, 0, HALF, CHUNK, last=True)
        for m in range(1, M_TILES):
            mm(B, 1, m, last=True)
        for m in range(M_TILES):
            gelu(A, m)
            if m % 2 == 1:
                store(A, m - 1, m + 1)
        x_copy(V, C, 0, 0, HALF)
        x_copy(V, C, 0, HALF, CHUNK)
        x_quant(C, 0, 0, HALF)
        x_quant(C, 0, HALF, CHUNK)
        for m in range(3):
            open_acc(C, m, m)
            mm(C, 0, m, first=True)
        for m in range(3):
            gelu(B, m)
            if m == 1:
                store(B, 0, 2)
        x_copy(S, C, 1, HALF + QUARTER, CHUNK)
        gelu(B, 3)
        store(B, 2, 4)
        x_copy(V, C, 1, 0, HALF)
        x_copy(V, C, 1, HALF, HALF + QUARTER)
        x_quant(C, 1, 0, HALF)
        x_quant(C, 1, HALF, CHUNK)
        mm(C, 1, 0, 0, HALF)
        mm(C, 1, 0, HALF, CHUNK, last=True)
        gelu(C, 0)
        store(C, 0, 1)
        for m in range(1, 3):
            mm(C, 1, m, last=True)
            gelu(C, m)
            store(C, m, m + 1)
        for g0 in (0, HALF):
            open_acc(C, 3, 3 + g0 // HALF, g0, g0 + HALF)
            mm(C, 0, 3, g0, g0 + HALF, g0, first=True)
            mm(C, 1, 3, g0, g0 + HALF, g0, last=True)
            gelu(C, 3, g0, g0 + HALF)
            store(C, 3, 4, g0, g0 + HALF)
